import numpy as np
import ml_dtypes


def mxq(x, axis, fmt="e4m3"):
    dtype, down = {"e4m3": (ml_dtypes.float8_e4m3fn, 7), "e5m2": (ml_dtypes.float8_e5m2, 14)}[fmt]
    v = np.moveaxis(np.asarray(x, np.float32).astype(ml_dtypes.bfloat16).astype(np.float64), axis, -1)
    blocks = v.reshape(v.shape[:-1] + (-1, 32))
    amax = np.abs(blocks).max(-1, keepdims=True)
    byte = np.maximum(np.where(amax > 0, np.frexp(amax)[1] - 1 + 127, 0) - down, 1)
    scale = np.exp2(byte - 127.0)
    codes = (blocks / scale).astype(np.float32).astype(dtype).astype(np.float64)
    return np.moveaxis((codes * scale).reshape(v.shape), -1, axis)


WIDE = False


def mx_kscale(k, group=512):
    if not WIDE:
        return np.ones(k)
    levels = np.array([10, -10, 5, -5, 0])
    if group != 512:
        return np.exp2(np.random.permutation(np.resize(levels, k // group))).repeat(group)
    if k % 512:
        return np.exp2(np.random.permutation(np.resize(levels, k // 32))).repeat(32)
    a = np.empty((k // 512, 16))
    for p in range(k // 512):
        a[p, :8] = np.random.permutation(np.resize(levels, 8))
        for g in range(8):
            far = levels[np.abs(levels - a[p, g]) >= 10]
            a[p, g + 8] = far[np.random.randint(len(far))]
    return np.exp2(a.ravel()).repeat(32)


def f64(x):
    return np.asarray(x).astype(np.float64)


def striped(idx):
    return np.tile(np.asarray(idx).reshape(-1, 16).T, (8, 1)).astype(np.uint16)


def unstriped(offs):
    return offs[:16].T.reshape(-1).astype(np.int64)


H, KV, D, NQ, N = 4, 1, 128, 512, 512


def setup_inputs():
    n = np.random.standard_normal
    s = mx_kscale(D, 0)[:, None]
    u = mx_kscale(N)
    t = np.random.uniform(0.5, 2.0, N) * u
    v = n((KV, N, 128))
    return {
        "qT": (n((H, D, NQ)) * s * (0.70 / np.sqrt(D))).astype(np.float32),
        "kT": (n((KV, D, N)) / s).astype(np.float32),
        "t": t.reshape(N, 1).astype(np.float32),
        "v": (v / t[:, None]).astype(np.float32),
        "kb": (0.5 * n((N, 1))).astype(np.float32),
        "mask": (np.arange(N)[:, None] <= np.sort(np.random.randint(N // 4, N, NQ))[None, :]).astype(np.float32),
        "gn": np.tile(np.random.uniform(0.5, 2.0, 128), (128, 1)).astype(np.float32),
    }


def reference(qT, kT, t, v, kb, mask, gn):
    a = np.repeat(mxq(f64(kT), 1, "e4m3"), H // KV, 0).transpose(0, 2, 1) @ mxq(f64(qT), 1, "e4m3")
    a = a + f64(kb)
    p = a / (1.0 + np.exp(-a))
    p = p * f64(mask)
    w = p * f64(t)
    y = mxq(w, 1, "e4m3").transpose(0, 2, 1) @ np.repeat(mxq(f64(v), 1, "e4m3"), H // KV, 0)
    y = y / 16.0
    y = y / np.sqrt(np.mean(np.square(y), -1, keepdims=True) + 1e-5) * f64(gn)[:1]
    return y

@@ -1,0 +1,170 @@
+from contextlib import ExitStack
+
+import concourse.mybir as mybir
+
+H, D, NQ, N, E = 4, 128, 512, 512, 128
+FLOPS = 2 * H * N * NQ * (D + E)
+
+F32 = mybir.dt.float32
+BF16 = mybir.dt.bfloat16
+U32 = mybir.dt.uint32
+U8 = mybir.dt.uint8
+FP8X4 = mybir.dt.float8_e4m3fn_x4
+ACT = mybir.ActivationFunctionType
+ALU = mybir.AluOpType
+
+P = 128
+R = 32
+PACK = 4
+QH = 256
+T = 128
+K_VEC = 84
+Q_VEC = 128
+
+
+def tile_rows_a_silu_kb_mask_onorm_kernel(tc, qT, kT, t, v, kb, mask, gn, out):
+    nc = tc.nc
+    with ExitStack() as ctx:
+        sb = ctx.enter_context(tc.tile_pool(name="sb", bufs=1))
+        ps = ctx.enter_context(tc.psum_pool(name="ps", bufs=1))
+        ctx.enter_context(tc.manual_schedule())
+
+        def mk(name, shape, dt):
+            return sb.tile(shape, dt, name=name, align_bytes=64)
+
+        k_raw = mk("k_raw", [P, PACK, N], F32)
+        q_raw = [mk("q_raw%d" % h, [P, PACK, QH], F32) for h in range(2)]
+        m_raw = [mk("m_raw%d" % h, [P, PACK, QH], F32) for h in range(2)]
+        v_raw = mk("v_raw", [P, PACK, E], F32)
+        t_sb = mk("t_sb", [P, PACK], F32)
+        kb_sb = mk("kb_sb", [P, PACK], F32)
+        gn_sb = mk("gn_sb", [P, E], F32)
+
+        k_src = kT[0].rearrange("(p j) n -> p j n", j=PACK)
+        q_src = qT.rearrange("h (p j) n -> (h p) j n", j=PACK)
+        m_src = mask.rearrange("(p r) n -> p r n", r=PACK)
+        for g in range(H):
+            eng = nc.sync if g < 2 else nc.scalar
+            eng.dma_start(out=k_raw[R * g : R * (g + 1)], in_=k_src)
+        nc.sync.dma_start(out=q_raw[0][:], in_=q_src[:, :, 0:QH])
+        nc.scalar.dma_start(out=kb_sb[:], in_=kb.rearrange("(p r) o -> p (r o)", r=PACK))
+        nc.scalar.dma_start(out=t_sb[:], in_=t.rearrange("(p r) o -> p (r o)", r=PACK))
+        nc.sync.dma_start(out=m_raw[0][:], in_=m_src[:, :, 0:QH])
+        nc.sync.dma_start(out=q_raw[1][:], in_=q_src[:, :, QH:NQ])
+        nc.sync.dma_start(out=m_raw[1][:], in_=m_src[:, :, QH:NQ])
+        nc.sync.dma_start(out=v_raw[:], in_=v[0].rearrange("(p j) e -> p j e", j=PACK))
+        nc.sync.dma_start(out=gn_sb[:], in_=gn)
+
+        warm_in = mk("warm_in", [P, 1], F32)
+        warm_out = mk("warm_out", [P, 1], F32)
+        nc.vector.memset(warm_in[:], 0.0)
+        nc.scalar.activation(out=warm_out[:], in_=warm_in[:], func=ACT.Silu)
+
+        def quantize(name, grouped, width):
+            codes = mk(name + "_codes", [P, width], U32)
+            scales = mk(name + "_scales", [P, width], U8)
+            nc.vector.quantize_mx(out=codes[:].bitcast(FP8X4), scales=scales[:], in_=grouped[:])
+            return codes, scales
+
+        def interleave(copy, grouped, raw, c0, c1):
+            dst = grouped[:].rearrange("p (c i j) -> p c j i", i=4, j=PACK)
+            src = raw[:].rearrange("p j (c i) -> p c j i", i=4)
+            copy(out=dst[:, c0 // 4 : c1 // 4], in_=src[:, c0 // 4 : c1 // 4])
+
+        k_bf = mk("k_bf", [P, N * PACK], BF16)
+        k_dst = k_bf[:].rearrange("p (r s j) -> p s j r", r=PACK, j=PACK)
+        k_in = k_raw[:].rearrange("p j (s r) -> p s j r", r=PACK)
+        nc.vector.tensor_copy(out=k_dst[:, 0:K_VEC], in_=k_in[:, 0:K_VEC])
+        nc.scalar.copy(out=k_dst[:, K_VEC:P], in_=k_in[:, K_VEC:P])
+        k_codes, k_scales = quantize("k", k_bf, N)
+
+        q_bf = [mk("q_bf%d" % h, [P, QH * PACK], BF16) for h in range(2)]
+        interleave(nc.scalar.copy, q_bf[0], q_raw[0], Q_VEC, QH)
+        interleave(nc.vector.tensor_copy, q_bf[0], q_raw[0], 0, Q_VEC)
+        q_mx = [quantize("q0", q_bf[0], QH)]
+
+        mt = [mk("mt%d" % h, [P, PACK, QH], F32) for h in range(2)]
+
+        def mask_times_t(h):
+            for r in range(PACK):
+                nc.vector.tensor_scalar(out=mt[h][:, r, :], in0=m_raw[h][:, r, :], scalar1=t_sb[:, r : r + 1], scalar2=None, op0=ALU.mult)
+
+        mask_times_t(0)
+        interleave(nc.vector.tensor_copy, q_bf[1], q_raw[1], 0, QH)
+        mask_times_t(1)
+        q_mx.append(quantize("q1", q_bf[1], QH))
+        v_bf = mk("v_bf", [P, E * PACK], BF16)
+        interleave(nc.vector.tensor_copy, v_bf, v_raw, 0, E)
+
+        s_bank = [ps.tile([P, 2, QH], F32, name="s_bank%d" % g) for g in range(H)]
+        y_bank = [ps.tile([P, 4, E], F32, name="y_bank%d" % b) for b in range(4)]
+        U = 2 * H
+        p_sb = [mk("p%d" % u, [P, PACK, QH], F32) for u in range(U)]
+
+        def fill(u, part):
+            h, g = divmod(u, H)
+            rows = slice(R * g, R * (g + 1))
+            q_codes, q_scales = q_mx[h]
+            for rr in range(2):
+                r = 2 * part + rr
+                kc = slice(T * r, T * (r + 1))
+                for tt in range(2):
+                    qc = slice(T * tt, T * (tt + 1))
+                    nc.tensor.matmul_mx(
+                        out=s_bank[g][:, rr, qc],
+                        lhsT=k_codes[rows, kc].bitcast(FP8X4), lhsT_scale=k_scales[rows, kc],
+                        rhs=q_codes[rows, qc].bitcast(FP8X4), rhs_scale=q_scales[rows, qc],
+                        start=True, stop=True)
+            for rr in range(2):
+                r = 2 * part + rr
+                nc.scalar.activation(out=p_sb[u][:, r, :], in_=s_bank[g][:, rr, :], func=ACT.Silu, bias=kb_sb[:, r : r + 1])
+
+        LEAD = 3
+        for step in range(U + LEAD):
+            if step >= LEAD:
+                fill(step - LEAD, 1)
+            if step < U:
+                fill(step, 0)
+
+        w_bf = [mk("w_bf%d" % u, [P, QH * PACK], BF16) for u in range(U)]
+
+        def weigh(u):
+            h = u // H
+            nc.vector.tensor_tensor(
+                out=w_bf[u][:].rearrange("p (c i r) -> p c r i", i=4, r=PACK),
+                in0=p_sb[u][:].rearrange("p r (c i) -> p c r i", i=4),
+                in1=mt[h][:].rearrange("p r (c i) -> p c r i", i=4),
+                op=ALU.mult)
+
+        def second(u):
+            w_codes, w_scales = quantize("w%d" % u, w_bf[u], QH)
+            for tt in range(2):
+                qc = slice(T * tt, T * (tt + 1))
+                nc.tensor.matmul_mx(
+                    out=y_bank[u // 2][:, 2 * (u % 2) + tt, :],
+                    lhsT=w_codes[:, qc].bitcast(FP8X4), lhsT_scale=w_scales[:, qc],
+                    rhs=v_codes[:].bitcast(FP8X4), rhs_scale=v_scales[:],
+                    start=True, stop=True)
+
+        weigh(0)
+        v_codes, v_scales = quantize("v", v_bf, E)
+        for u in range(1, U):
+            weigh(u)
+            second(u - 1)
+        second(U - 1)
+
+        squares = mk("squares", [P, 16, E], F32)
+        ssq = mk("ssq", [P, 16], F32)
+        rinv = mk("rinv", [P, 16], F32)
+        res = [mk("res%d" % u, [P, 2, E], F32) for u in range(U)]
+        for b in range(4):
+            for i in range(4):
+                nc.scalar.activation(out=squares[:, 4 * b + i, :], in_=y_bank[b][:, i, :], func=ACT.Square, accum_out=ssq[:, 4 * b + i : 4 * b + i + 1])
+            nc.scalar.activation(out=rinv[:, 4 * b : 4 * b + 4], in_=ssq[:, 4 * b : 4 * b + 4], func=ACT.Abs_reciprocal_sqrt, scale=1.0 / E, bias=256.0 * 1e-5)
+            for uu in range(2):
+                u = 2 * b + uu
+                h, g = divmod(u, H)
+                for tt in range(2):
+                    i = 2 * uu + tt
+                    nc.vector.scalar_tensor_tensor(out=res[u][:, tt, :], in0=y_bank[b][:, i, :], scalar=rinv[:, 4 * b + i : 4 * b + i + 1], in1=gn_sb[:], op0=ALU.mult, op1=ALU.mult)
+                nc.sync.dma_start(out=out[g, QH * h : QH * (h + 1), :].rearrange("(t p) e -> p t e", p=P), in_=res[u][:])

@@ -7,7 +7,7 @@ FLOPS = 2 * H * N * NQ * (D + E)
 
 F32 = mybir.dt.float32
 BF16 = mybir.dt.bfloat16
-U32 = mybir.dt.uint32
+I32 = mybir.dt.int32
 U8 = mybir.dt.uint8
 FP8X4 = mybir.dt.float8_e4m3fn_x4
 ACT = mybir.ActivationFunctionType
@@ -20,6 +20,7 @@ QH = 256
 T = 128
 K_VEC = 84
 Q_VEC = 128
+HEADS = (0, 2, 1, 3)
 
 
 def tile_rows_a_silu_kb_mask_onorm_kernel(tc, qT, kT, t, v, kb, mask, gn, out):
@@ -32,7 +33,7 @@ def tile_rows_a_silu_kb_mask_onorm_kernel(tc, qT, kT, t, v, kb, mask, gn, out):
         def mk(name, shape, dt):
             return sb.tile(shape, dt, name=name, align_bytes=64)
 
-        k_raw = mk("k_raw", [P, PACK, N], F32)
+        k_raw = mk("k_raw", [P, PACK * N], F32)
         q_raw = [mk("q_raw%d" % h, [P, PACK, QH], F32) for h in range(2)]
         m_raw = [mk("m_raw%d" % h, [P, PACK, QH], F32) for h in range(2)]
         v_raw = mk("v_raw", [P, PACK, E], F32)
@@ -40,43 +41,50 @@ def tile_rows_a_silu_kb_mask_onorm_kernel(tc, qT, kT, t, v, kb, mask, gn, out):
         kb_sb = mk("kb_sb", [P, PACK], F32)
         gn_sb = mk("gn_sb", [P, E], F32)
 
-        k_src = kT[0].rearrange("(p j) n -> p j n", j=PACK)
+        k_src = kT[0].rearrange("(p j) n -> p (j n)", j=PACK)
         q_src = qT.rearrange("h (p j) n -> (h p) j n", j=PACK)
         m_src = mask.rearrange("(p r) n -> p r n", r=PACK)
-        for g in range(H):
-            eng = nc.sync if g < 2 else nc.scalar
-            eng.dma_start(out=k_raw[R * g : R * (g + 1)], in_=k_src)
+        nc.sync.dma_start(out=k_raw[0:R], in_=k_src)
+        nc.scalar.dma_start(out=k_raw[2 * R : 3 * R], in_=k_src)
         nc.sync.dma_start(out=q_raw[0][:], in_=q_src[:, :, 0:QH])
         nc.scalar.dma_start(out=kb_sb[:], in_=kb.rearrange("(p r) o -> p (r o)", r=PACK))
         nc.scalar.dma_start(out=t_sb[:], in_=t.rearrange("(p r) o -> p (r o)", r=PACK))
         nc.sync.dma_start(out=m_raw[0][:], in_=m_src[:, :, 0:QH])
-        nc.sync.dma_start(out=q_raw[1][:], in_=q_src[:, :, QH:NQ])
-        nc.sync.dma_start(out=m_raw[1][:], in_=m_src[:, :, QH:NQ])
         nc.sync.dma_start(out=v_raw[:], in_=v[0].rearrange("(p j) e -> p j e", j=PACK))
-        nc.sync.dma_start(out=gn_sb[:], in_=gn)
 
         warm_in = mk("warm_in", [P, 1], F32)
         warm_out = mk("warm_out", [P, 1], F32)
         nc.vector.memset(warm_in[:], 0.0)
         nc.scalar.activation(out=warm_out[:], in_=warm_in[:], func=ACT.Silu)
+        k_mx = mk("k_mx", [P, N + N // 4], I32)
+        nc.vector.memset(k_raw[R : 2 * R, :].bitcast(I32), 0)
+        nc.vector.memset(k_mx[:, N : N + N // 4], 0)
 
         def quantize(name, grouped, width):
-            codes = mk(name + "_codes", [P, width], U32)
+            codes = mk(name + "_codes", [P, width], I32)
             scales = mk(name + "_scales", [P, width], U8)
             nc.vector.quantize_mx(out=codes[:].bitcast(FP8X4), scales=scales[:], in_=grouped[:])
             return codes, scales
 
         def interleave(copy, grouped, raw, c0, c1):
-            dst = grouped[:].rearrange("p (c i j) -> p c j i", i=4, j=PACK)
-            src = raw[:].rearrange("p j (c i) -> p c j i", i=4)
-            copy(out=dst[:, c0 // 4 : c1 // 4], in_=src[:, c0 // 4 : c1 // 4])
+            dst = grouped[:].rearrange("p (c i j) -> p c j i", i=2, j=PACK)
+            src = raw[:].rearrange("p j (c i) -> p c j i", i=2)
+            copy(out=dst[:, c0 // 2 : c1 // 2], in_=src[:, c0 // 2 : c1 // 2])
 
+        KP = 3 * R
         k_bf = mk("k_bf", [P, N * PACK], BF16)
         k_dst = k_bf[:].rearrange("p (r s j) -> p s j r", r=PACK, j=PACK)
-        k_in = k_raw[:].rearrange("p j (s r) -> p s j r", r=PACK)
-        nc.vector.tensor_copy(out=k_dst[:, 0:K_VEC], in_=k_in[:, 0:K_VEC])
-        nc.scalar.copy(out=k_dst[:, K_VEC:P], in_=k_in[:, K_VEC:P])
-        k_codes, k_scales = quantize("k", k_bf, N)
+        k_in = k_raw[:].rearrange("p (j s r) -> p s j r", j=PACK, r=PACK)
+        nc.vector.tensor_copy(out=k_dst[0:KP, 0:K_VEC], in_=k_in[0:KP, 0:K_VEC])
+        nc.scalar.copy(out=k_dst[0:KP, K_VEC:P], in_=k_in[0:KP, K_VEC:P])
+        k_codes = k_mx[:, 0:N]
+        k_scales = k_mx[:, N : N + N // 4].bitcast(U8)
+        nc.vector.quantize_mx(out=k_codes[0:KP].bitcast(FP8X4), scales=k_scales[0:KP], in_=k_bf[0:KP, :])
+        nc.sync.dma_start(out=k_mx[R : 2 * R, :], in_=k_mx[0:R, :])
+        nc.sync.dma_start(out=k_mx[3 * R : 4 * R, :], in_=k_mx[2 * R : 3 * R, :])
+        nc.sync.dma_start(out=q_raw[1][:], in_=q_src[:, :, QH:NQ])
+        nc.sync.dma_start(out=m_raw[1][:], in_=m_src[:, :, QH:NQ])
+        nc.sync.dma_start(out=gn_sb[:], in_=gn)
 
         q_bf = [mk("q_bf%d" % h, [P, QH * PACK], BF16) for h in range(2)]
         interleave(nc.scalar.copy, q_bf[0], q_raw[0], Q_VEC, QH)
@@ -89,82 +97,88 @@ def tile_rows_a_silu_kb_mask_onorm_kernel(tc, qT, kT, t, v, kb, mask, gn, out):
             for r in range(PACK):
                 nc.vector.tensor_scalar(out=mt[h][:, r, :], in0=m_raw[h][:, r, :], scalar1=t_sb[:, r : r + 1], scalar2=None, op0=ALU.mult)
 
-        mask_times_t(0)
-        interleave(nc.vector.tensor_copy, q_bf[1], q_raw[1], 0, QH)
-        mask_times_t(1)
-        q_mx.append(quantize("q1", q_bf[1], QH))
+        s_bank = [ps.tile([P, PACK, T], F32, name="s_bank%d" % g) for g in range(H)]
+        y_bank = [ps.tile([P, H, E], F32, name="y_bank%d" % b) for b in range(4)]
+        U = 16
+        p_sb = [mk("p%d" % u, [P, PACK, T], F32) for u in range(U)]
+        w_bf = [mk("w_bf%d" % n, [P, 2 * T * PACK], BF16) for n in range(U // 2)]
         v_bf = mk("v_bf", [P, E * PACK], BF16)
-        interleave(nc.vector.tensor_copy, v_bf, v_raw, 0, E)
+        w_mx = {}
 
-        s_bank = [ps.tile([P, 2, QH], F32, name="s_bank%d" % g) for g in range(H)]
-        y_bank = [ps.tile([P, 4, E], F32, name="y_bank%d" % b) for b in range(4)]
-        U = 2 * H
-        p_sb = [mk("p%d" % u, [P, PACK, QH], F32) for u in range(U)]
-
-        def fill(u, part):
-            h, g = divmod(u, H)
+        def scores(u):
+            c, g = u // H, HEADS[u % H]
             rows = slice(R * g, R * (g + 1))
-            q_codes, q_scales = q_mx[h]
-            for rr in range(2):
-                r = 2 * part + rr
+            q_codes, q_scales = q_mx[c // 2]
+            qc = slice(T * (c % 2), T * (c % 2 + 1))
+            for r in range(PACK):
                 kc = slice(T * r, T * (r + 1))
-                for tt in range(2):
-                    qc = slice(T * tt, T * (tt + 1))
-                    nc.tensor.matmul_mx(
-                        out=s_bank[g][:, rr, qc],
-                        lhsT=k_codes[rows, kc].bitcast(FP8X4), lhsT_scale=k_scales[rows, kc],
-                        rhs=q_codes[rows, qc].bitcast(FP8X4), rhs_scale=q_scales[rows, qc],
-                        start=True, stop=True)
-            for rr in range(2):
-                r = 2 * part + rr
-                nc.scalar.activation(out=p_sb[u][:, r, :], in_=s_bank[g][:, rr, :], func=ACT.Silu, bias=kb_sb[:, r : r + 1])
-
-        LEAD = 3
-        for step in range(U + LEAD):
-            if step >= LEAD:
-                fill(step - LEAD, 1)
-            if step < U:
-                fill(step, 0)
-
-        w_bf = [mk("w_bf%d" % u, [P, QH * PACK], BF16) for u in range(U)]
+                nc.tensor.matmul_mx(
+                    out=s_bank[g][:, r, :],
+                    lhsT=k_codes[rows, kc].bitcast(FP8X4), lhsT_scale=k_scales[rows, kc],
+                    rhs=q_codes[rows, qc].bitcast(FP8X4), rhs_scale=q_scales[rows, qc],
+                    start=True, stop=True)
+            for r in range(PACK):
+                nc.scalar.activation(out=p_sb[u][:, r, :], in_=s_bank[g][:, r, :], func=ACT.Silu, bias=kb_sb[:, r : r + 1])
 
         def weigh(u):
-            h = u // H
+            c = u // H
+            half = slice(T * PACK * (u % 2), T * PACK * (u % 2 + 1))
             nc.vector.tensor_tensor(
-                out=w_bf[u][:].rearrange("p (c i r) -> p c r i", i=4, r=PACK),
-                in0=p_sb[u][:].rearrange("p r (c i) -> p c r i", i=4),
-                in1=mt[h][:].rearrange("p r (c i) -> p c r i", i=4),
+                out=w_bf[u // 2][:, half].rearrange("p (c i r) -> p c r i", i=2, r=PACK),
+                in0=p_sb[u][:].rearrange("p r (c i) -> p c r i", i=2),
+                in1=mt[c // 2][:, :, T * (c % 2) : T * (c % 2 + 1)].rearrange("p r (c i) -> p c r i", i=2),
                 op=ALU.mult)
 
-        def second(u):
-            w_codes, w_scales = quantize("w%d" % u, w_bf[u], QH)
-            for tt in range(2):
-                qc = slice(T * tt, T * (tt + 1))
+        def quantize_w(n):
+            return quantize("w%d" % n, w_bf[n], 2 * T)
+
+        def second(n, w_pair):
+            w_codes, w_scales = w_pair
+            for uu in range(2):
+                u = 2 * n + uu
+                qc = slice(T * uu, T * (uu + 1))
                 nc.tensor.matmul_mx(
-                    out=y_bank[u // 2][:, 2 * (u % 2) + tt, :],
+                    out=y_bank[u // H][:, u % H, :],
                     lhsT=w_codes[:, qc].bitcast(FP8X4), lhsT_scale=w_scales[:, qc],
                     rhs=v_codes[:].bitcast(FP8X4), rhs_scale=v_scales[:],
                     start=True, stop=True)
 
+        mask_times_t(0)
+        for u in range(U // 2):
+            scores(u)
         weigh(0)
+        interleave(nc.vector.tensor_copy, v_bf, v_raw, 0, E)
+        weigh(1)
         v_codes, v_scales = quantize("v", v_bf, E)
-        for u in range(1, U):
+        weigh(2)
+        interleave(nc.vector.tensor_copy, q_bf[1], q_raw[1], 0, QH)
+        w_all = [quantize_w(0)]
+        q_mx.append(quantize("q1", q_bf[1], QH))
+        for u in range(U // 2, U):
+            scores(u)
+        for u in range(3, U):
             weigh(u)
-            second(u - 1)
-        second(U - 1)
+            if u % 2 == 0:
+                w_all.append(quantize_w(u // 2 - 1))
+            if u == 5:
+                mask_times_t(1)
+        for n in range(U // 2 - 1):
+            second(n, w_all[n])
 
-        squares = mk("squares", [P, 16, E], F32)
-        ssq = mk("ssq", [P, 16], F32)
-        rinv = mk("rinv", [P, 16], F32)
-        res = [mk("res%d" % u, [P, 2, E], F32) for u in range(U)]
+        squares = mk("squares", [P, U, E], F32)
+        ssq = mk("ssq", [P, U], F32)
+        rinv = mk("rinv", [P, U], F32)
+        res = [mk("res%d" % n, [P, 2, E], F32) for n in range(U // 2)]
+        out_v = out.rearrange("(a b) (c p) e -> b c p a e", b=2, p=P)
         for b in range(4):
-            for i in range(4):
-                nc.scalar.activation(out=squares[:, 4 * b + i, :], in_=y_bank[b][:, i, :], func=ACT.Square, accum_out=ssq[:, 4 * b + i : 4 * b + i + 1])
-            nc.scalar.activation(out=rinv[:, 4 * b : 4 * b + 4], in_=ssq[:, 4 * b : 4 * b + 4], func=ACT.Abs_reciprocal_sqrt, scale=1.0 / E, bias=256.0 * 1e-5)
-            for uu in range(2):
-                u = 2 * b + uu
-                h, g = divmod(u, H)
-                for tt in range(2):
-                    i = 2 * uu + tt
-                    nc.vector.scalar_tensor_tensor(out=res[u][:, tt, :], in0=y_bank[b][:, i, :], scalar=rinv[:, 4 * b + i : 4 * b + i + 1], in1=gn_sb[:], op0=ALU.mult, op1=ALU.mult)
-                nc.sync.dma_start(out=out[g, QH * h : QH * (h + 1), :].rearrange("(t p) e -> p t e", p=P), in_=res[u][:])
+            if b == 1:
+                second(U // 2 - 1, quantize_w(U // 2 - 1))
+            for i in range(H):
+                nc.scalar.activation(out=squares[:, H * b + i, :], in_=y_bank[b][:, i, :], func=ACT.Square, accum_out=ssq[:, H * b + i : H * b + i + 1])
+            nc.scalar.activation(out=rinv[:, H * b : H * b + H], in_=ssq[:, H * b : H * b + H], func=ACT.Abs_reciprocal_sqrt, scale=1.0 / E, bias=256.0 * 1e-5)
+            for nn in range(2):
+                n = 2 * b + nn
+                for uu in range(2):
+                    u = 2 * n + uu
+                    nc.vector.scalar_tensor_tensor(out=res[n][:, uu, :], in0=y_bank[b][:, u % H, :], scalar=rinv[:, u : u + 1], in1=gn_sb[:], op0=ALU.mult, op1=ALU.mult)
+                nc.sync.dma_start(out=out_v[nn, b], in_=res[n][:])

@@ -19,7 +19,7 @@ PACK = 4
 QH = 256
 T = 128
 K_VEC = 84
-Q_VEC = 128
+Q_VEC = 48
 HEADS = (0, 2, 1, 3)
 
 
@@ -45,7 +45,6 @@ def tile_rows_a_silu_kb_mask_onorm_kernel(tc, qT, kT, t, v, kb, mask, gn, out):
         q_src = qT.rearrange("h (p j) n -> (h p) j n", j=PACK)
         m_src = mask.rearrange("(p r) n -> p r n", r=PACK)
         nc.sync.dma_start(out=k_raw[0:R], in_=k_src)
-        nc.scalar.dma_start(out=k_raw[2 * R : 3 * R], in_=k_src)
         nc.sync.dma_start(out=q_raw[0][:], in_=q_src[:, :, 0:QH])
         nc.scalar.dma_start(out=kb_sb[:], in_=kb.rearrange("(p r) o -> p (r o)", r=PACK))
         nc.scalar.dma_start(out=t_sb[:], in_=t.rearrange("(p r) o -> p (r o)", r=PACK))
@@ -57,13 +56,12 @@ def tile_rows_a_silu_kb_mask_onorm_kernel(tc, qT, kT, t, v, kb, mask, gn, out):
         nc.vector.memset(warm_in[:], 0.0)
         nc.scalar.activation(out=warm_out[:], in_=warm_in[:], func=ACT.Silu)
         k_mx = mk("k_mx", [P, N + N // 4], I32)
-        nc.vector.memset(k_raw[R : 2 * R, :].bitcast(I32), 0)
-        nc.vector.memset(k_mx[:, N : N + N // 4], 0)
+        nc.vector.memset(k_mx[0:R, N : N + N // 4], 0)
 
         def quantize(name, grouped, width):
             codes = mk(name + "_codes", [P, width], I32)
             scales = mk(name + "_scales", [P, width], U8)
-            nc.vector.quantize_mx(out=codes[:].bitcast(FP8X4), scales=scales[:], in_=grouped[:])
+            nc.vector.quantize_mx(out=codes[:].bitcast(FP8X4), scales=scales[:], in_=grouped)
             return codes, scales
 
         def interleave(copy, grouped, raw, c0, c1):
@@ -71,7 +69,7 @@ def tile_rows_a_silu_kb_mask_onorm_kernel(tc, qT, kT, t, v, kb, mask, gn, out):
             src = raw[:].rearrange("p j (c i) -> p c j i", i=2)
             copy(out=dst[:, c0 // 2 : c1 // 2], in_=src[:, c0 // 2 : c1 // 2])
 
-        KP = 3 * R
+        KP = R
         k_bf = mk("k_bf", [P, N * PACK], BF16)
         k_dst = k_bf[:].rearrange("p (r s j) -> p s j r", r=PACK, j=PACK)
         k_in = k_raw[:].rearrange("p (j s r) -> p s j r", j=PACK, r=PACK)
@@ -80,16 +78,18 @@ def tile_rows_a_silu_kb_mask_onorm_kernel(tc, qT, kT, t, v, kb, mask, gn, out):
         k_codes = k_mx[:, 0:N]
         k_scales = k_mx[:, N : N + N // 4].bitcast(U8)
         nc.vector.quantize_mx(out=k_codes[0:KP].bitcast(FP8X4), scales=k_scales[0:KP], in_=k_bf[0:KP, :])
-        nc.sync.dma_start(out=k_mx[R : 2 * R, :], in_=k_mx[0:R, :])
-        nc.sync.dma_start(out=k_mx[3 * R : 4 * R, :], in_=k_mx[2 * R : 3 * R, :])
+        for g in HEADS[1:]:
+            nc.sync.dma_start(out=k_mx[R * g : R * (g + 1), :], in_=k_mx[0:R, :])
         nc.sync.dma_start(out=q_raw[1][:], in_=q_src[:, :, QH:NQ])
         nc.sync.dma_start(out=m_raw[1][:], in_=m_src[:, :, QH:NQ])
         nc.sync.dma_start(out=gn_sb[:], in_=gn)
 
         q_bf = [mk("q_bf%d" % h, [P, QH * PACK], BF16) for h in range(2)]
-        interleave(nc.scalar.copy, q_bf[0], q_raw[0], Q_VEC, QH)
+        interleave(nc.scalar.copy, q_bf[0], q_raw[0], Q_VEC, T)
         interleave(nc.vector.tensor_copy, q_bf[0], q_raw[0], 0, Q_VEC)
-        q_mx = [quantize("q0", q_bf[0], QH)]
+        q_mx = [quantize("q0", q_bf[0][:, 0 : T * PACK], T)]
+        interleave(nc.scalar.copy, q_bf[0], q_raw[0], T, QH)
+        q_mx.append(quantize("q1", q_bf[0][:, T * PACK : QH * PACK], T))
 
         mt = [mk("mt%d" % h, [P, PACK, QH], F32) for h in range(2)]
 
@@ -97,88 +97,109 @@ def tile_rows_a_silu_kb_mask_onorm_kernel(tc, qT, kT, t, v, kb, mask, gn, out):
             for r in range(PACK):
                 nc.vector.tensor_scalar(out=mt[h][:, r, :], in0=m_raw[h][:, r, :], scalar1=t_sb[:, r : r + 1], scalar2=None, op0=ALU.mult)
 
-        s_bank = [ps.tile([P, PACK, T], F32, name="s_bank%d" % g) for g in range(H)]
+        s_bank = [ps.tile([P, PACK * T], F32, name="s_bank%d" % g) for g in range(H)]
         y_bank = [ps.tile([P, H, E], F32, name="y_bank%d" % b) for b in range(4)]
-        U = 16
-        p_sb = [mk("p%d" % u, [P, PACK, T], F32) for u in range(U)]
-        w_bf = [mk("w_bf%d" % n, [P, 2 * T * PACK], BF16) for n in range(U // 2)]
+        U = 2 * H
+        p_sb = [mk("p%d" % u, [P, PACK, QH], F32) for u in range(U)]
+        w_bf = [mk("w_bf%d" % u, [P, QH * PACK], BF16) for u in range(U)]
         v_bf = mk("v_bf", [P, E * PACK], BF16)
-        w_mx = {}
 
-        def scores(u):
-            c, g = u // H, HEADS[u % H]
+        def scores(g, q_pair, places, p_out):
             rows = slice(R * g, R * (g + 1))
-            q_codes, q_scales = q_mx[c // 2]
-            qc = slice(T * (c % 2), T * (c % 2 + 1))
-            for r in range(PACK):
+            q_codes, q_scales = q_pair
+            width = PACK * T // len(places)
+            for n, r in enumerate(places):
                 kc = slice(T * r, T * (r + 1))
-                nc.tensor.matmul_mx(
-                    out=s_bank[g][:, r, :],
-                    lhsT=k_codes[rows, kc].bitcast(FP8X4), lhsT_scale=k_scales[rows, kc],
-                    rhs=q_codes[rows, qc].bitcast(FP8X4), rhs_scale=q_scales[rows, qc],
-                    start=True, stop=True)
-            for r in range(PACK):
-                nc.scalar.activation(out=p_sb[u][:, r, :], in_=s_bank[g][:, r, :], func=ACT.Silu, bias=kb_sb[:, r : r + 1])
+                for c in range(0, width, T):
+                    nc.tensor.matmul_mx(
+                        out=s_bank[g][:, n * width + c : n * width + c + T],
+                        lhsT=k_codes[rows, kc].bitcast(FP8X4), lhsT_scale=k_scales[rows, kc],
+                        rhs=q_codes[rows, c : c + T].bitcast(FP8X4), rhs_scale=q_scales[rows, c : c + T],
+                        start=True, stop=True)
+            for n, r in enumerate(places):
+                nc.scalar.activation(out=p_out[:, r, :], in_=s_bank[g][:, n * width : (n + 1) * width], func=ACT.Silu, bias=kb_sb[:, r : r + 1])
 
-        def weigh(u):
-            c = u // H
-            half = slice(T * PACK * (u % 2), T * PACK * (u % 2 + 1))
+        def weigh(u, c0, c1):
             nc.vector.tensor_tensor(
-                out=w_bf[u // 2][:, half].rearrange("p (c i r) -> p c r i", i=2, r=PACK),
-                in0=p_sb[u][:].rearrange("p r (c i) -> p c r i", i=2),
-                in1=mt[c // 2][:, :, T * (c % 2) : T * (c % 2 + 1)].rearrange("p r (c i) -> p c r i", i=2),
+                out=w_bf[u][:, PACK * c0 : PACK * c1].rearrange("p (c i r) -> p c r i", i=2, r=PACK),
+                in0=p_sb[u][:, :, c0:c1].rearrange("p r (c i) -> p c r i", i=2),
+                in1=mt[u // H][:, :, c0:c1].rearrange("p r (c i) -> p c r i", i=2),
                 op=ALU.mult)
 
-        def quantize_w(n):
-            return quantize("w%d" % n, w_bf[n], 2 * T)
+        w_mx = {}
 
-        def second(n, w_pair):
-            w_codes, w_scales = w_pair
-            for uu in range(2):
-                u = 2 * n + uu
-                qc = slice(T * uu, T * (uu + 1))
+        def quantize_w(u):
+            w_mx.setdefault(u, quantize("w%d" % u, w_bf[u][:], QH))
+
+        def y_tile(u, c):
+            b, half = divmod(u, 2)
+            return y_bank[b][:, 2 * half + c, :]
+
+        def second(u):
+            w_codes, w_scales = w_mx[u]
+            for c in range(2):
+                qc = slice(T * c, T * (c + 1))
                 nc.tensor.matmul_mx(
-                    out=y_bank[u // H][:, u % H, :],
+                    out=y_tile(u, c),
                     lhsT=w_codes[:, qc].bitcast(FP8X4), lhsT_scale=w_scales[:, qc],
                     rhs=v_codes[:].bitcast(FP8X4), rhs_scale=v_scales[:],
                     start=True, stop=True)
 
         mask_times_t(0)
-        for u in range(U // 2):
-            scores(u)
-        weigh(0)
-        interleave(nc.vector.tensor_copy, v_bf, v_raw, 0, E)
-        weigh(1)
-        v_codes, v_scales = quantize("v", v_bf, E)
-        weigh(2)
-        interleave(nc.vector.tensor_copy, q_bf[1], q_raw[1], 0, QH)
-        w_all = [quantize_w(0)]
-        q_mx.append(quantize("q1", q_bf[1], QH))
-        for u in range(U // 2, U):
-            scores(u)
-        for u in range(3, U):
-            weigh(u)
-            if u % 2 == 0:
-                w_all.append(quantize_w(u // 2 - 1))
-            if u == 5:
-                mask_times_t(1)
-        for n in range(U // 2 - 1):
-            second(n, w_all[n])
+        NARROW = [(u, c) for c in range(2) for u in range(H)]
+        for u, c in NARROW:
+            scores(HEADS[u], q_mx[c], range(PACK), p_sb[u][:, :, T * c : T * (c + 1)])
 
-        squares = mk("squares", [P, U, E], F32)
-        ssq = mk("ssq", [P, U], F32)
-        rinv = mk("rinv", [P, U], F32)
-        res = [mk("res%d" % n, [P, 2, E], F32) for n in range(U // 2)]
-        out_v = out.rearrange("(a b) (c p) e -> b c p a e", b=2, p=P)
-        for b in range(4):
-            if b == 1:
-                second(U // 2 - 1, quantize_w(U // 2 - 1))
-            for i in range(H):
-                nc.scalar.activation(out=squares[:, H * b + i, :], in_=y_bank[b][:, i, :], func=ACT.Square, accum_out=ssq[:, H * b + i : H * b + i + 1])
-            nc.scalar.activation(out=rinv[:, H * b : H * b + H], in_=ssq[:, H * b : H * b + H], func=ACT.Abs_reciprocal_sqrt, scale=1.0 / E, bias=256.0 * 1e-5)
-            for nn in range(2):
-                n = 2 * b + nn
-                for uu in range(2):
-                    u = 2 * n + uu
-                    nc.vector.scalar_tensor_tensor(out=res[n][:, uu, :], in0=y_bank[b][:, u % H, :], scalar=rinv[:, u : u + 1], in1=gn_sb[:], op0=ALU.mult, op1=ALU.mult)
-                nc.sync.dma_start(out=out_v[nn, b], in_=res[n][:])
+        def weigh_narrow(n):
+            u, c = NARROW[n]
+            weigh(u, T * c, T * (c + 1))
+
+        interleave(nc.vector.tensor_copy, v_bf, v_raw, 0, E)
+        weigh_narrow(0)
+        v_codes, v_scales = quantize("v", v_bf[:], E)
+        weigh_narrow(1)
+        interleave(nc.vector.tensor_copy, q_bf[1], q_raw[1], 0, QH)
+        weigh_narrow(2)
+        q_wide = quantize("q2", q_bf[1][:], QH)
+        for n in range(3, 8):
+            weigh_narrow(n)
+            if n > 4:
+                quantize_w(n - 5)
+        mask_times_t(1)
+        quantize_w(3)
+        for u, places in ((0, (0, 1)), (1, (0, 1)), (2, (0, 1)), (0, (2, 3)), (3, (0, 1)), (1, (2, 3)), (2, (2, 3)), (3, (2, 3))):
+            scores(HEADS[u], q_wide, places, p_sb[H + u])
+        for u in range(H, U):
+            weigh(u, 0, QH)
+            if u > H:
+                quantize_w(u - 1)
+        quantize_w(U - 1)
+
+        squares = mk("squares", [P, 2 * U, E], F32)
+        ssq = mk("ssq", [P, 2 * U], F32)
+        rinv = mk("rinv", [P, 2 * U], F32)
+        res = [mk("res%d" % u, [P, 2, E], F32) for u in range(U)]
+        out_v = out.rearrange("h (a c p) e -> a h p c e", c=2, p=P)
+
+        def square(u):
+            for c in range(2):
+                i = 2 * u + c
+                nc.scalar.activation(out=squares[:, i, :], in_=y_tile(u, c), func=ACT.Square, accum_out=ssq[:, i : i + 1])
+
+        def root(u0, u1):
+            nc.scalar.activation(out=rinv[:, 2 * u0 : 2 * u1], in_=ssq[:, 2 * u0 : 2 * u1], func=ACT.Abs_reciprocal_sqrt, scale=1.0 / E, bias=256.0 * 1e-5)
+
+        def norm(u):
+            for c in range(2):
+                i = 2 * u + c
+                nc.vector.scalar_tensor_tensor(out=res[u][:, c, :], in0=y_tile(u, c), scalar=rinv[:, i : i + 1], in1=gn_sb[:], op0=ALU.mult, op1=ALU.mult)
+            nc.sync.dma_start(out=out_v[u // H, HEADS[u % H]], in_=res[u][:])
+
+        for u in range(U):
+            second(u)
+        for u in range(U):
+            square(u)
+            if u % 2 == 1:
+                root(u - 1, u + 1)
+        for u in range(U):
+            norm(u)

@@ -14,13 +14,16 @@ ACT = mybir.ActivationFunctionType
 ALU = mybir.AluOpType
 
 P = 128
-R = 32
-PACK = 4
-QH = 256
-T = 128
-K_VEC = 84
-Q_VEC = 48
+ROWS = D // 4
+PLACES = 4
+COLS = 128
+HALF = NQ // 2
+UNITS = 2 * H
+BANK = 512
 HEADS = (0, 2, 1, 3)
+K_ON_VECTOR = 84
+Q_ON_VECTOR = 48
+EPS = 16.0 * 16.0 * 1e-5
 
 
 def tile_rows_a_silu_kb_mask_onorm_kernel(tc, qT, kT, t, v, kb, mask, gn, out):
@@ -30,176 +33,169 @@ def tile_rows_a_silu_kb_mask_onorm_kernel(tc, qT, kT, t, v, kb, mask, gn, out):
         ps = ctx.enter_context(tc.psum_pool(name="ps", bufs=1))
         ctx.enter_context(tc.manual_schedule())
 
-        def mk(name, shape, dt):
-            return sb.tile(shape, dt, name=name, align_bytes=64)
+        def sbuf(name, shape, dtype):
+            return sb.tile(shape, dtype, name=name, align_bytes=64)
 
-        k_raw = mk("k_raw", [P, PACK * N], F32)
-        q_raw = [mk("q_raw%d" % h, [P, PACK, QH], F32) for h in range(2)]
-        m_raw = [mk("m_raw%d" % h, [P, PACK, QH], F32) for h in range(2)]
-        v_raw = mk("v_raw", [P, PACK, E], F32)
-        t_sb = mk("t_sb", [P, PACK], F32)
-        kb_sb = mk("kb_sb", [P, PACK], F32)
-        gn_sb = mk("gn_sb", [P, E], F32)
-
-        k_src = kT[0].rearrange("(p j) n -> p (j n)", j=PACK)
-        q_src = qT.rearrange("h (p j) n -> (h p) j n", j=PACK)
-        m_src = mask.rearrange("(p r) n -> p r n", r=PACK)
-        nc.sync.dma_start(out=k_raw[0:R], in_=k_src)
-        nc.sync.dma_start(out=q_raw[0][:], in_=q_src[:, :, 0:QH])
-        nc.scalar.dma_start(out=kb_sb[:], in_=kb.rearrange("(p r) o -> p (r o)", r=PACK))
-        nc.scalar.dma_start(out=t_sb[:], in_=t.rearrange("(p r) o -> p (r o)", r=PACK))
-        nc.sync.dma_start(out=m_raw[0][:], in_=m_src[:, :, 0:QH])
-        nc.sync.dma_start(out=v_raw[:], in_=v[0].rearrange("(p j) e -> p j e", j=PACK))
-
-        warm_in = mk("warm_in", [P, 1], F32)
-        warm_out = mk("warm_out", [P, 1], F32)
-        nc.vector.memset(warm_in[:], 0.0)
-        nc.scalar.activation(out=warm_out[:], in_=warm_in[:], func=ACT.Silu)
-        k_mx = mk("k_mx", [P, N + N // 4], I32)
-        nc.vector.memset(k_mx[0:R, N : N + N // 4], 0)
-
-        def quantize(name, grouped, width):
-            codes = mk(name + "_codes", [P, width], I32)
-            scales = mk(name + "_scales", [P, width], U8)
-            nc.vector.quantize_mx(out=codes[:].bitcast(FP8X4), scales=scales[:], in_=grouped)
+        def quantize(name, packed, words):
+            codes = sbuf(name + "_codes", [P, words], I32)
+            scales = sbuf(name + "_scales", [P, words], U8)
+            nc.vector.quantize_mx(out=codes[:].bitcast(FP8X4), scales=scales[:], in_=packed)
             return codes, scales
 
-        def interleave(copy, grouped, raw, c0, c1):
-            dst = grouped[:].rearrange("p (c i j) -> p c j i", i=2, j=PACK)
+        def pack(copy, packed, raw, first, last):
+            dst = packed[:].rearrange("p (c i j) -> p c j i", i=2, j=PLACES)
             src = raw[:].rearrange("p j (c i) -> p c j i", i=2)
-            copy(out=dst[:, c0 // 2 : c1 // 2], in_=src[:, c0 // 2 : c1 // 2])
+            copy(out=dst[:, first // 2 : last // 2], in_=src[:, first // 2 : last // 2])
 
-        KP = R
-        k_bf = mk("k_bf", [P, N * PACK], BF16)
-        k_dst = k_bf[:].rearrange("p (r s j) -> p s j r", r=PACK, j=PACK)
-        k_in = k_raw[:].rearrange("p (j s r) -> p s j r", j=PACK, r=PACK)
-        nc.vector.tensor_copy(out=k_dst[0:KP, 0:K_VEC], in_=k_in[0:KP, 0:K_VEC])
-        nc.scalar.copy(out=k_dst[0:KP, K_VEC:P], in_=k_in[0:KP, K_VEC:P])
+        k_raw = sbuf("k_raw", [ROWS, PLACES * N], F32)
+        q_raw = [sbuf("q_raw%d" % a, [P, PLACES, HALF], F32) for a in range(2)]
+        mask_raw = [sbuf("mask_raw%d" % a, [P, PLACES, HALF], F32) for a in range(2)]
+        v_raw = sbuf("v_raw", [P, PLACES, E], F32)
+        t_sb = sbuf("t_sb", [P, PLACES], F32)
+        kb_sb = sbuf("kb_sb", [P, PLACES], F32)
+        gn_sb = sbuf("gn_sb", [P, E], F32)
+        q_src = qT.rearrange("h (p j) n -> (h p) j n", j=PLACES)
+        mask_src = mask.rearrange("(s r) n -> s r n", r=PLACES)
+        nc.sync.dma_start(out=k_raw[:], in_=kT[0].rearrange("(p j) n -> p (j n)", j=PLACES))
+        nc.sync.dma_start(out=q_raw[0][:], in_=q_src[:, :, 0:HALF])
+        nc.sync.dma_start(out=mask_raw[0][:], in_=mask_src[:, :, 0:HALF])
+        nc.sync.dma_start(out=v_raw[:], in_=v[0].rearrange("(s r) e -> s r e", r=PLACES))
+
+        warm_in = sbuf("warm_in", [P, 1], F32)
+        warm_out = sbuf("warm_out", [P, 1], F32)
+        nc.vector.memset(warm_in[:], 0.0)
+        nc.scalar.activation(out=warm_out[:], in_=warm_in[:], func=ACT.Silu)
+        nc.scalar.dma_start(out=kb_sb[:], in_=kb.rearrange("(s r) o -> s (r o)", r=PLACES))
+        nc.scalar.dma_start(out=t_sb[:], in_=t.rearrange("(s r) o -> s (r o)", r=PLACES))
+
+        k_mx = sbuf("k_mx", [P, N + N // 4], I32)
         k_codes = k_mx[:, 0:N]
         k_scales = k_mx[:, N : N + N // 4].bitcast(U8)
-        nc.vector.quantize_mx(out=k_codes[0:KP].bitcast(FP8X4), scales=k_scales[0:KP], in_=k_bf[0:KP, :])
+        nc.vector.memset(k_mx[0:ROWS, N : N + N // 4], 0)
+        k_packed = sbuf("k_packed", [ROWS, N * PLACES], BF16)
+        k_dst = k_packed[:].rearrange("p (r s j) -> p s j r", r=PLACES, j=PLACES)
+        k_src = k_raw[:].rearrange("p (j s r) -> p s j r", j=PLACES, r=PLACES)
+        nc.vector.tensor_copy(out=k_dst[:, 0:K_ON_VECTOR], in_=k_src[:, 0:K_ON_VECTOR])
+        nc.scalar.copy(out=k_dst[:, K_ON_VECTOR:P], in_=k_src[:, K_ON_VECTOR:P])
+        nc.vector.quantize_mx(out=k_codes[0:ROWS].bitcast(FP8X4), scales=k_scales[0:ROWS], in_=k_packed[:])
         for g in HEADS[1:]:
-            nc.sync.dma_start(out=k_mx[R * g : R * (g + 1), :], in_=k_mx[0:R, :])
-        nc.sync.dma_start(out=q_raw[1][:], in_=q_src[:, :, QH:NQ])
-        nc.sync.dma_start(out=m_raw[1][:], in_=m_src[:, :, QH:NQ])
+            nc.sync.dma_start(out=k_mx[ROWS * g : ROWS * (g + 1), :], in_=k_mx[0:ROWS, :])
+        nc.sync.dma_start(out=q_raw[1][:], in_=q_src[:, :, HALF:NQ])
+        nc.sync.dma_start(out=mask_raw[1][:], in_=mask_src[:, :, HALF:NQ])
         nc.sync.dma_start(out=gn_sb[:], in_=gn)
 
-        q_bf = [mk("q_bf%d" % h, [P, QH * PACK], BF16) for h in range(2)]
-        interleave(nc.scalar.copy, q_bf[0], q_raw[0], Q_VEC, T)
-        interleave(nc.vector.tensor_copy, q_bf[0], q_raw[0], 0, Q_VEC)
-        q_mx = [quantize("q0", q_bf[0][:, 0 : T * PACK], T)]
-        interleave(nc.scalar.copy, q_bf[0], q_raw[0], T, QH)
-        q_mx.append(quantize("q1", q_bf[0][:, T * PACK : QH * PACK], T))
+        q_packed = [sbuf("q_packed%d" % a, [P, HALF * PLACES], BF16) for a in range(2)]
+        pack(nc.scalar.copy, q_packed[0], q_raw[0], Q_ON_VECTOR, COLS)
+        pack(nc.vector.tensor_copy, q_packed[0], q_raw[0], 0, Q_ON_VECTOR)
+        q_quarters = [quantize("q_quarter0", q_packed[0][:, 0 : COLS * PLACES], COLS)]
+        pack(nc.scalar.copy, q_packed[0], q_raw[0], COLS, HALF)
+        q_quarters.append(quantize("q_quarter1", q_packed[0][:, COLS * PLACES : HALF * PLACES], COLS))
 
-        mt = [mk("mt%d" % h, [P, PACK, QH], F32) for h in range(2)]
+        score_bank = [ps.tile([P, BANK], F32, name="score_bank%d" % g) for g in range(H)]
+        y_bank = [ps.tile([P, 4, E], F32, name="y_bank%d" % b) for b in range(UNITS // 2)]
+        mask_t = [sbuf("mask_t%d" % a, [P, PLACES, HALF], F32) for a in range(2)]
+        p_sb = [sbuf("p%d" % u, [P, PLACES, HALF], F32) for u in range(UNITS)]
+        w_packed = [sbuf("w_packed%d" % u, [P, HALF * PLACES], BF16) for u in range(UNITS)]
+        v_packed = sbuf("v_packed", [P, E * PLACES], BF16)
+        squares = sbuf("squares", [P, 2 * UNITS, E], F32)
+        sum_sq = sbuf("sum_sq", [P, 2 * UNITS], F32)
+        inv_rms = sbuf("inv_rms", [P, 2 * UNITS], F32)
+        result = [sbuf("result%d" % u, [P, 2, E], F32) for u in range(UNITS)]
+        out_units = out.rearrange("h (a m c) e -> a h m c e", c=2, m=P)
+        w_mx = []
 
-        def mask_times_t(h):
-            for r in range(PACK):
-                nc.vector.tensor_scalar(out=mt[h][:, r, :], in0=m_raw[h][:, r, :], scalar1=t_sb[:, r : r + 1], scalar2=None, op0=ALU.mult)
+        def mask_times_t(a):
+            for r in range(PLACES):
+                nc.vector.tensor_scalar(
+                    out=mask_t[a][:, r, :], in0=mask_raw[a][:, r, :], scalar1=t_sb[:, r : r + 1], scalar2=None,
+                    op0=ALU.mult)
 
-        s_bank = [ps.tile([P, PACK * T], F32, name="s_bank%d" % g) for g in range(H)]
-        y_bank = [ps.tile([P, H, E], F32, name="y_bank%d" % b) for b in range(4)]
-        U = 2 * H
-        p_sb = [mk("p%d" % u, [P, PACK, QH], F32) for u in range(U)]
-        w_bf = [mk("w_bf%d" % u, [P, QH * PACK], BF16) for u in range(U)]
-        v_bf = mk("v_bf", [P, E * PACK], BF16)
-
-        def scores(g, q_pair, places, p_out):
-            rows = slice(R * g, R * (g + 1))
-            q_codes, q_scales = q_pair
-            width = PACK * T // len(places)
+        def scores(g, q_mx, places, p_out):
+            rows = slice(ROWS * g, ROWS * (g + 1))
+            q_codes, q_scales = q_mx
+            width = BANK // len(places)
             for n, r in enumerate(places):
-                kc = slice(T * r, T * (r + 1))
-                for c in range(0, width, T):
+                keys = slice(COLS * r, COLS * (r + 1))
+                for first in range(0, width, COLS):
                     nc.tensor.matmul_mx(
-                        out=s_bank[g][:, n * width + c : n * width + c + T],
-                        lhsT=k_codes[rows, kc].bitcast(FP8X4), lhsT_scale=k_scales[rows, kc],
-                        rhs=q_codes[rows, c : c + T].bitcast(FP8X4), rhs_scale=q_scales[rows, c : c + T],
+                        out=score_bank[g][:, n * width + first : n * width + first + COLS],
+                        lhsT=k_codes[rows, keys].bitcast(FP8X4), lhsT_scale=k_scales[rows, keys],
+                        rhs=q_codes[rows, first : first + COLS].bitcast(FP8X4),
+                        rhs_scale=q_scales[rows, first : first + COLS],
                         start=True, stop=True)
             for n, r in enumerate(places):
-                nc.scalar.activation(out=p_out[:, r, :], in_=s_bank[g][:, n * width : (n + 1) * width], func=ACT.Silu, bias=kb_sb[:, r : r + 1])
+                nc.scalar.activation(
+                    out=p_out[:, r, :], in_=score_bank[g][:, n * width : (n + 1) * width], func=ACT.Silu,
+                    bias=kb_sb[:, r : r + 1])
 
-        def weigh(u, c0, c1):
+        def weigh(u, first, last):
             nc.vector.tensor_tensor(
-                out=w_bf[u][:, PACK * c0 : PACK * c1].rearrange("p (c i r) -> p c r i", i=2, r=PACK),
-                in0=p_sb[u][:, :, c0:c1].rearrange("p r (c i) -> p c r i", i=2),
-                in1=mt[u // H][:, :, c0:c1].rearrange("p r (c i) -> p c r i", i=2),
+                out=w_packed[u][:].rearrange("s (c m r) -> s m r c", c=2, r=PLACES)[:, first // 2 : last // 2],
+                in0=p_sb[u][:, :, first:last].rearrange("s r (m c) -> s m r c", c=2),
+                in1=mask_t[u // H][:, :, first:last].rearrange("s r (m c) -> s m r c", c=2),
                 op=ALU.mult)
 
-        w_mx = {}
-
         def quantize_w(u):
-            w_mx.setdefault(u, quantize("w%d" % u, w_bf[u][:], QH))
+            w_mx.append(quantize("w%d" % u, w_packed[u][:], HALF))
 
         def y_tile(u, c):
-            b, half = divmod(u, 2)
-            return y_bank[b][:, 2 * half + c, :]
+            return y_bank[u // 2][:, 2 * (u % 2) + c, :]
 
-        def second(u):
+        quarter_steps = [(u, c) for c in range(2) for u in range(H)]
+        mask_times_t(0)
+        for u, c in quarter_steps:
+            scores(HEADS[u], q_quarters[c], range(PLACES), p_sb[u][:, :, COLS * c : COLS * (c + 1)])
+
+        def weigh_step(n):
+            u, c = quarter_steps[n]
+            weigh(u, COLS * c, COLS * (c + 1))
+
+        pack(nc.vector.tensor_copy, v_packed, v_raw, 0, E)
+        weigh_step(0)
+        v_codes, v_scales = quantize("v", v_packed[:], E)
+        weigh_step(1)
+        pack(nc.vector.tensor_copy, q_packed[1], q_raw[1], 0, HALF)
+        weigh_step(2)
+        q_second = quantize("q_second", q_packed[1][:], HALF)
+        for n in range(3, len(quarter_steps)):
+            weigh_step(n)
+            if n > H:
+                quantize_w(n - H - 1)
+        mask_times_t(1)
+        quantize_w(H - 1)
+
+        half_steps = [(u, places) for places in ((0, 1), (2, 3)) for u in range(H)]
+        half_steps[H - 1 : H + 1] = [half_steps[H], half_steps[H - 1]]
+        for u, places in half_steps:
+            scores(HEADS[u], q_second, places, p_sb[H + u])
+        for u in range(H, UNITS):
+            weigh(u, 0, HALF)
+            if u > H:
+                quantize_w(u - 1)
+        quantize_w(UNITS - 1)
+
+        for u in range(UNITS):
             w_codes, w_scales = w_mx[u]
             for c in range(2):
-                qc = slice(T * c, T * (c + 1))
+                queries = slice(COLS * c, COLS * (c + 1))
                 nc.tensor.matmul_mx(
                     out=y_tile(u, c),
-                    lhsT=w_codes[:, qc].bitcast(FP8X4), lhsT_scale=w_scales[:, qc],
+                    lhsT=w_codes[:, queries].bitcast(FP8X4), lhsT_scale=w_scales[:, queries],
                     rhs=v_codes[:].bitcast(FP8X4), rhs_scale=v_scales[:],
                     start=True, stop=True)
 
-        mask_times_t(0)
-        NARROW = [(u, c) for c in range(2) for u in range(H)]
-        for u, c in NARROW:
-            scores(HEADS[u], q_mx[c], range(PACK), p_sb[u][:, :, T * c : T * (c + 1)])
-
-        def weigh_narrow(n):
-            u, c = NARROW[n]
-            weigh(u, T * c, T * (c + 1))
-
-        interleave(nc.vector.tensor_copy, v_bf, v_raw, 0, E)
-        weigh_narrow(0)
-        v_codes, v_scales = quantize("v", v_bf[:], E)
-        weigh_narrow(1)
-        interleave(nc.vector.tensor_copy, q_bf[1], q_raw[1], 0, QH)
-        weigh_narrow(2)
-        q_wide = quantize("q2", q_bf[1][:], QH)
-        for n in range(3, 8):
-            weigh_narrow(n)
-            if n > 4:
-                quantize_w(n - 5)
-        mask_times_t(1)
-        quantize_w(3)
-        for u, places in ((0, (0, 1)), (1, (0, 1)), (2, (0, 1)), (0, (2, 3)), (3, (0, 1)), (1, (2, 3)), (2, (2, 3)), (3, (2, 3))):
-            scores(HEADS[u], q_wide, places, p_sb[H + u])
-        for u in range(H, U):
-            weigh(u, 0, QH)
-            if u > H:
-                quantize_w(u - 1)
-        quantize_w(U - 1)
-
-        squares = mk("squares", [P, 2 * U, E], F32)
-        ssq = mk("ssq", [P, 2 * U], F32)
-        rinv = mk("rinv", [P, 2 * U], F32)
-        res = [mk("res%d" % u, [P, 2, E], F32) for u in range(U)]
-        out_v = out.rearrange("h (a c p) e -> a h p c e", c=2, p=P)
-
-        def square(u):
+        for b in range(UNITS // 2):
+            for i in range(4 * b, 4 * b + 4):
+                nc.scalar.activation(
+                    out=squares[:, i, :], in_=y_tile(i // 2, i % 2), func=ACT.Square,
+                    accum_out=sum_sq[:, i : i + 1])
+            nc.scalar.activation(
+                out=inv_rms[:, 4 * b : 4 * b + 4], in_=sum_sq[:, 4 * b : 4 * b + 4],
+                func=ACT.Abs_reciprocal_sqrt, scale=1.0 / E, bias=EPS)
+        for u in range(UNITS):
             for c in range(2):
                 i = 2 * u + c
-                nc.scalar.activation(out=squares[:, i, :], in_=y_tile(u, c), func=ACT.Square, accum_out=ssq[:, i : i + 1])
-
-        def root(u0, u1):
-            nc.scalar.activation(out=rinv[:, 2 * u0 : 2 * u1], in_=ssq[:, 2 * u0 : 2 * u1], func=ACT.Abs_reciprocal_sqrt, scale=1.0 / E, bias=256.0 * 1e-5)
-
-        def norm(u):
-            for c in range(2):
-                i = 2 * u + c
-                nc.vector.scalar_tensor_tensor(out=res[u][:, c, :], in0=y_tile(u, c), scalar=rinv[:, i : i + 1], in1=gn_sb[:], op0=ALU.mult, op1=ALU.mult)
-            nc.sync.dma_start(out=out_v[u // H, HEADS[u % H]], in_=res[u][:])
-
-        for u in range(U):
-            second(u)
-        for u in range(U):
-            square(u)
-            if u % 2 == 1:
-                root(u - 1, u + 1)
-        for u in range(U):
-            norm(u)
+                nc.vector.scalar_tensor_tensor(
+                    out=result[u][:, c, :], in0=y_tile(u, c), scalar=inv_rms[:, i : i + 1], in1=gn_sb[:],
+                    op0=ALU.mult, op1=ALU.mult)
+            nc.sync.dma_start(out=out_units[u // H, HEADS[u % H]], in_=result[u][:])

from contextlib import ExitStack

import concourse.mybir as mybir

H, D, NQ, N, E = 4, 128, 512, 512, 128
FLOPS = 2 * H * N * NQ * (D + E)

F32 = mybir.dt.float32
BF16 = mybir.dt.bfloat16
I32 = mybir.dt.int32
U8 = mybir.dt.uint8
FP8X4 = mybir.dt.float8_e4m3fn_x4
ACT = mybir.ActivationFunctionType
ALU = mybir.AluOpType

P = 128
ROWS = D // 4
PLACES = 4
COLS = 128
HALF = NQ // 2
UNITS = 2 * H
BANK = 512
HEADS = (0, 2, 1, 3)
K_ON_VECTOR = 84
Q_ON_VECTOR = 48
EPS = 16.0 * 16.0 * 1e-5


def tile_rows_a_silu_kb_mask_onorm_kernel(tc, qT, kT, t, v, kb, mask, gn, out):
    nc = tc.nc
    with ExitStack() as ctx:
        sb = ctx.enter_context(tc.tile_pool(name="sb", bufs=1))
        ps = ctx.enter_context(tc.psum_pool(name="ps", bufs=1))
        ctx.enter_context(tc.manual_schedule())

        def sbuf(name, shape, dtype):
            return sb.tile(shape, dtype, name=name, align_bytes=64)

        def quantize(name, packed, words):
            codes = sbuf(name + "_codes", [P, words], I32)
            scales = sbuf(name + "_scales", [P, words], U8)
            nc.vector.quantize_mx(out=codes[:].bitcast(FP8X4), scales=scales[:], in_=packed)
            return codes, scales

        def pack(copy, packed, raw, first, last):
            dst = packed[:].rearrange("p (c i j) -> p c j i", i=2, j=PLACES)
            src = raw[:].rearrange("p j (c i) -> p c j i", i=2)
            copy(out=dst[:, first // 2 : last // 2], in_=src[:, first // 2 : last // 2])

        k_raw = sbuf("k_raw", [ROWS, PLACES * N], F32)
        q_raw = [sbuf("q_raw%d" % a, [P, PLACES, HALF], F32) for a in range(2)]
        mask_raw = [sbuf("mask_raw%d" % a, [P, PLACES, HALF], F32) for a in range(2)]
        v_raw = sbuf("v_raw", [P, PLACES, E], F32)
        t_sb = sbuf("t_sb", [P, PLACES], F32)
        kb_sb = sbuf("kb_sb", [P, PLACES], F32)
        gn_sb = sbuf("gn_sb", [P, E], F32)
        q_src = qT.rearrange("h (p j) n -> (h p) j n", j=PLACES)
        mask_src = mask.rearrange("(s r) n -> s r n", r=PLACES)
        nc.sync.dma_start(out=k_raw[:], in_=kT[0].rearrange("(p j) n -> p (j n)", j=PLACES))
        nc.sync.dma_start(out=q_raw[0][:], in_=q_src[:, :, 0:HALF])
        nc.sync.dma_start(out=mask_raw[0][:], in_=mask_src[:, :, 0:HALF])
        nc.sync.dma_start(out=v_raw[:], in_=v[0].rearrange("(s r) e -> s r e", r=PLACES))

        warm_in = sbuf("warm_in", [P, 1], F32)
        warm_out = sbuf("warm_out", [P, 1], F32)
        nc.vector.memset(warm_in[:], 0.0)
        nc.scalar.activation(out=warm_out[:], in_=warm_in[:], func=ACT.Silu)
        nc.scalar.dma_start(out=kb_sb[:], in_=kb.rearrange("(s r) o -> s (r o)", r=PLACES))
        nc.scalar.dma_start(out=t_sb[:], in_=t.rearrange("(s r) o -> s (r o)", r=PLACES))

        k_mx = sbuf("k_mx", [P, N + N // 4], I32)
        k_codes = k_mx[:, 0:N]
        k_scales = k_mx[:, N : N + N // 4].bitcast(U8)
        nc.vector.memset(k_mx[0:ROWS, N : N + N // 4], 0)
        k_packed = sbuf("k_packed", [ROWS, N * PLACES], BF16)
        k_dst = k_packed[:].rearrange("p (r s j) -> p s j r", r=PLACES, j=PLACES)
        k_src = k_raw[:].rearrange("p (j s r) -> p s j r", j=PLACES, r=PLACES)
        nc.vector.tensor_copy(out=k_dst[:, 0:K_ON_VECTOR], in_=k_src[:, 0:K_ON_VECTOR])
        nc.scalar.copy(out=k_dst[:, K_ON_VECTOR:P], in_=k_src[:, K_ON_VECTOR:P])
        nc.vector.quantize_mx(out=k_codes[0:ROWS].bitcast(FP8X4), scales=k_scales[0:ROWS], in_=k_packed[:])
        for g in HEADS[1:]:
            nc.sync.dma_start(out=k_mx[ROWS * g : ROWS * (g + 1), :], in_=k_mx[0:ROWS, :])
        nc.sync.dma_start(out=q_raw[1][:], in_=q_src[:, :, HALF:NQ])
        nc.sync.dma_start(out=mask_raw[1][:], in_=mask_src[:, :, HALF:NQ])
        nc.sync.dma_start(out=gn_sb[:], in_=gn)

        q_packed = [sbuf("q_packed%d" % a, [P, HALF * PLACES], BF16) for a in range(2)]
        pack(nc.scalar.copy, q_packed[0], q_raw[0], Q_ON_VECTOR, COLS)
        pack(nc.vector.tensor_copy, q_packed[0], q_raw[0], 0, Q_ON_VECTOR)
        q_quarters = [quantize("q_quarter0", q_packed[0][:, 0 : COLS * PLACES], COLS)]
        pack(nc.scalar.copy, q_packed[0], q_raw[0], COLS, HALF)
        q_quarters.append(quantize("q_quarter1", q_packed[0][:, COLS * PLACES : HALF * PLACES], COLS))

        score_bank = [ps.tile([P, BANK], F32, name="score_bank%d" % g) for g in range(H)]
        y_bank = [ps.tile([P, 4, E], F32, name="y_bank%d" % b) for b in range(UNITS // 2)]
        mask_t = [sbuf("mask_t%d" % a, [P, PLACES, HALF], F32) for a in range(2)]
        p_sb = [sbuf("p%d" % u, [P, PLACES, HALF], F32) for u in range(UNITS)]
        w_packed = [sbuf("w_packed%d" % u, [P, HALF * PLACES], BF16) for u in range(UNITS)]
        v_packed = sbuf("v_packed", [P, E * PLACES], BF16)
        squares = sbuf("squares", [P, 2 * UNITS, E], F32)
        sum_sq = sbuf("sum_sq", [P, 2 * UNITS], F32)
        inv_rms = sbuf("inv_rms", [P, 2 * UNITS], F32)
        result = [sbuf("result%d" % u, [P, 2, E], F32) for u in range(UNITS)]
        out_units = out.rearrange("h (a m c) e -> a h m c e", c=2, m=P)
        w_mx = []

        def mask_times_t(a):
            for r in range(PLACES):
                nc.vector.tensor_scalar(
                    out=mask_t[a][:, r, :], in0=mask_raw[a][:, r, :], scalar1=t_sb[:, r : r + 1], scalar2=None,
                    op0=ALU.mult)

        def scores(g, q_mx, places, p_out):
            rows = slice(ROWS * g, ROWS * (g + 1))
            q_codes, q_scales = q_mx
            width = BANK // len(places)
            for n, r in enumerate(places):
                keys = slice(COLS * r, COLS * (r + 1))
                for first in range(0, width, COLS):
                    nc.tensor.matmul_mx(
                        out=score_bank[g][:, n * width + first : n * width + first + COLS],
                        lhsT=k_codes[rows, keys].bitcast(FP8X4), lhsT_scale=k_scales[rows, keys],
                        rhs=q_codes[rows, first : first + COLS].bitcast(FP8X4),
                        rhs_scale=q_scales[rows, first : first + COLS],
                        start=True, stop=True)
            for n, r in enumerate(places):
                nc.scalar.activation(
                    out=p_out[:, r, :], in_=score_bank[g][:, n * width : (n + 1) * width], func=ACT.Silu,
                    bias=kb_sb[:, r : r + 1])

        def weigh(u, first, last):
            nc.vector.tensor_tensor(
                out=w_packed[u][:].rearrange("s (c m r) -> s m r c", c=2, r=PLACES)[:, first // 2 : last // 2],
                in0=p_sb[u][:, :, first:last].rearrange("s r (m c) -> s m r c", c=2),
                in1=mask_t[u // H][:, :, first:last].rearrange("s r (m c) -> s m r c", c=2),
                op=ALU.mult)

        def quantize_w(u):
            w_mx.append(quantize("w%d" % u, w_packed[u][:], HALF))

        def y_tile(u, c):
            return y_bank[u // 2][:, 2 * (u % 2) + c, :]

        quarter_steps = [(u, c) for c in range(2) for u in range(H)]
        mask_times_t(0)
        for u, c in quarter_steps:
            scores(HEADS[u], q_quarters[c], range(PLACES), p_sb[u][:, :, COLS * c : COLS * (c + 1)])

        def weigh_step(n):
            u, c = quarter_steps[n]
            weigh(u, COLS * c, COLS * (c + 1))

        pack(nc.vector.tensor_copy, v_packed, v_raw, 0, E)
        weigh_step(0)
        v_codes, v_scales = quantize("v", v_packed[:], E)
        weigh_step(1)
        pack(nc.vector.tensor_copy, q_packed[1], q_raw[1], 0, HALF)
        weigh_step(2)
        q_second = quantize("q_second", q_packed[1][:], HALF)
        for n in range(3, len(quarter_steps)):
            weigh_step(n)
            if n > H:
                quantize_w(n - H - 1)
        mask_times_t(1)
        quantize_w(H - 1)

        half_steps = [(u, places) for places in ((0, 1), (2, 3)) for u in range(H)]
        half_steps[H - 1 : H + 1] = [half_steps[H], half_steps[H - 1]]
        for u, places in half_steps:
            scores(HEADS[u], q_second, places, p_sb[H + u])
        for u in range(H, UNITS):
            weigh(u, 0, HALF)
            if u > H:
                quantize_w(u - 1)
        quantize_w(UNITS - 1)

        for u in range(UNITS):
            w_codes, w_scales = w_mx[u]
            for c in range(2):
                queries = slice(COLS * c, COLS * (c + 1))
                nc.tensor.matmul_mx(
                    out=y_tile(u, c),
                    lhsT=w_codes[:, queries].bitcast(FP8X4), lhsT_scale=w_scales[:, queries],
                    rhs=v_codes[:].bitcast(FP8X4), rhs_scale=v_scales[:],
                    start=True, stop=True)

        for b in range(UNITS // 2):
            for i in range(4 * b, 4 * b + 4):
                nc.scalar.activation(
                    out=squares[:, i, :], in_=y_tile(i // 2, i % 2), func=ACT.Square,
                    accum_out=sum_sq[:, i : i + 1])
            nc.scalar.activation(
                out=inv_rms[:, 4 * b : 4 * b + 4], in_=sum_sq[:, 4 * b : 4 * b + 4],
                func=ACT.Abs_reciprocal_sqrt, scale=1.0 / E, bias=EPS)
        for u in range(UNITS):
            for c in range(2):
                i = 2 * u + c
                nc.vector.scalar_tensor_tensor(
                    out=result[u][:, c, :], in0=y_tile(u, c), scalar=inv_rms[:, i : i + 1], in1=gn_sb[:],
                    op0=ALU.mult, op1=ALU.mult)
            nc.sync.dma_start(out=out_units[u // H, HEADS[u % H]], in_=result[u][:])
